import numpy as np
import ml_dtypes


def mxq(x, axis, fmt="e4m3"):
    dtype, down = {"e4m3": (ml_dtypes.float8_e4m3fn, 7), "e5m2": (ml_dtypes.float8_e5m2, 14)}[fmt]
    v = np.moveaxis(np.asarray(x, np.float32).astype(ml_dtypes.bfloat16).astype(np.float64), axis, -1)
    blocks = v.reshape(v.shape[:-1] + (-1, 32))
    amax = np.abs(blocks).max(-1, keepdims=True)
    byte = np.maximum(np.where(amax > 0, np.frexp(amax)[1] - 1 + 127, 0) - down, 1)
    scale = np.exp2(byte - 127.0)
    codes = (blocks / scale).astype(np.float32).astype(dtype).astype(np.float64)
    return np.moveaxis((codes * scale).reshape(v.shape), -1, axis)


WIDE = False


def mx_kscale(k):
    if not WIDE:
        return np.ones(k)
    levels = np.array([10, -10, 5, -5, 0])
    if k % 512:
        return np.exp2(np.random.permutation(np.resize(levels, k // 32))).repeat(32)
    a = np.empty((k // 512, 16))
    for p in range(k // 512):
        a[p, :8] = np.random.permutation(np.resize(levels, 8))
        for g in range(8):
            far = levels[np.abs(levels - a[p, g]) >= 10]
            a[p, g + 8] = far[np.random.randint(len(far))]
    return np.exp2(a.ravel()).repeat(32)


def f64(x):
    return np.asarray(x).astype(np.float64)


def striped(idx):
    return np.tile(np.asarray(idx).reshape(-1, 16).T, (8, 1)).astype(np.uint16)


def unstriped(offs):
    return offs[:16].T.reshape(-1).astype(np.int64)


E2M1 = np.array([0.0, 0.5, 1.0, 1.5, 2.0, 3.0, 4.0, 6.0, -0.0, -0.5, -1.0, -1.5, -2.0, -3.0, -4.0, -6.0])


def pack_weight(w, fmt):
    k, n = w.shape
    w = f64(np.asarray(w, np.float32).astype(ml_dtypes.bfloat16)).reshape(k // 32, 32, n)
    amax = np.abs(w).max(1)
    if fmt == "e4m3":
        byte = np.frexp(amax)[1] - 1 + 127 - 7
    else:
        mant, ex = np.frexp(amax / 6.0)
        byte = np.where(mant > 0.5, ex, ex - 1) + 127
    byte = np.clip(np.where(amax > 0, byte, 1), 1, 254)
    scaled = (w * np.exp2(127.0 - byte)[:, None, :]).reshape(k, n).astype(np.float32)
    by_word = np.ascontiguousarray(scaled.reshape(k // 512, 128, 4, n).transpose(0, 1, 3, 2))
    if fmt == "e4m3":
        words = by_word.astype(ml_dtypes.float8_e4m3fn).view(np.uint8)
    else:
        c = by_word.astype(ml_dtypes.float4_e2m1fn).view(np.uint8) & 0xF
        words = (c[..., 0::2] | (c[..., 1::2] << 4)).reshape(k // 512, 128, 2 * n)
    return np.ascontiguousarray(words), np.ascontiguousarray(byte.astype(np.uint8).reshape(k // 512, 16, n))


def unpack_weight(words, scales, fmt):
    g, _, n = scales.shape
    words = np.ascontiguousarray(words).reshape(g, 128, n, -1)
    if fmt == "e4m3":
        vals = words.view(ml_dtypes.float8_e4m3fn).astype(np.float64)
    else:
        nib = np.empty((g, 128, n, 4), np.uint8)
        nib[..., 0::2] = words & 0xF
        nib[..., 1::2] = words >> 4
        vals = E2M1[nib]
    vals = vals * np.repeat(np.exp2(scales.astype(np.float64) - 127.0), 8, axis=1)[..., None]
    return vals.transpose(0, 1, 3, 2).reshape(g * 512, n)


def softplus(v):
    return np.log(1.0 + np.exp(v))


def sigmoid(v):
    return 1.0 / (1.0 + np.exp(-v))


D, E, T, I, Q, G = 512, 512, 2048, 512, 128, 64


def setup_inputs():
    n = np.random.standard_normal
    idx = np.random.permutation(T)[:I]
    fd = mx_kscale(D)
    fi = mx_kscale(I)
    ti = np.ones(T)
    ti[idx] = fi
    keysp = pack_weight(n((D, T)) / fd[:, None], "e2m1")
    return {
        "query": (n((D, Q)) * 0.8 / np.sqrt(D) * fd[:, None]).astype(np.float32),
        "query2": (n((D, Q)) * 1.0 / np.sqrt(D) * fd[:, None]).astype(np.float32),
        "keys_words": keysp[0],
        "keys_scales": keysp[1],
        "reserve": (np.random.uniform(2.0, 10.0, (Q, 1))).astype(np.float32),
        "dquery2": (n((D, Q)) * 0.6 / np.sqrt(D) * fd[:, None]).astype(np.float32),
        "os": (np.random.uniform(4.0, 16.0, (1, I)) * fi).astype(np.float32),
        "vals": (n((E, T)) / ti).astype(np.float32),
        "offs": striped(idx),
    }


def reference(query, query2, keys_words, keys_scales, reserve, dquery2, os, vals, offs):
    idx = unstriped(offs)
    keysu = unpack_weight(keys_words, keys_scales, "e2m1")
    queryq = mxq(f64(query), 0, "e4m3")
    keysidxg = keysu[:, idx]
    a = queryq.T @ keysidxg
    query2q = mxq(f64(query2), 0, "e4m3")
    b = query2q.T @ keysidxg
    dquery2q = mxq(f64(dquery2), 0, "e4m3")
    tb = dquery2q.T @ keysidxg
    m1 = b.reshape(Q, G, I // G).mean(axis=2)
    q0 = softplus(m1 * 3.0)
    z = np.sum(q0, axis=1, keepdims=True) + f64(reserve)
    pa = np.exp(a)
    s = pa.reshape(Q, G, I // G).sum(axis=2)
    tm1 = tb.reshape(Q, G, I // G).mean(axis=2)
    tq0 = tm1 * 3.0 * sigmoid(m1 * 3.0)
    tz = np.sum(tq0, axis=1, keepdims=True)
    tr = (tq0 / s - tz * q0 / s / z) / z
    trr = np.repeat(tr, I // G, axis=1)
    tw = trr * pa
    wo1 = tw * f64(os)
    wt1 = wo1.T
    vt1 = f64(vals)[:, idx].T
    wt1q = mxq(wt1, 0, "e4m3")
    vt1q = mxq(vt1, 0, "e4m3")
    o = wt1q.T @ vt1q
    return o

@@ -1,0 +1,201 @@
+from contextlib import ExitStack
+
+import concourse.mybir as mybir
+from concourse.masks import make_identity
+
+D, E, T, I, Q, G = 512, 512, 2048, 512, 128, 64
+FLOPS = 2 * Q * I * D * 3 + 2 * Q * I * E
+
+F32 = mybir.dt.float32
+BF16 = mybir.dt.bfloat16
+I32 = mybir.dt.int32
+U32 = mybir.dt.uint32
+U16 = mybir.dt.uint16
+U8 = mybir.dt.uint8
+FP8X4 = mybir.dt.float8_e4m3fn_x4
+FP4X4 = mybir.dt.float4_e2m1fn_x4
+ACT = mybir.ActivationFunctionType
+ALU = mybir.AluOpType
+AX = mybir.AxisListType
+
+P = 128
+PACK = 4
+PAGE = I // G
+TILES = E // P
+
+
+def tile_attend_ttpagequotas_kernel(tc, query, query2, keys_words, keys_scales, reserve, dquery2, slot_factor, vals, offs, out):
+    nc = tc.nc
+    with ExitStack() as ctx:
+        sb = ctx.enter_context(tc.tile_pool(name="sb", bufs=1))
+        ps = ctx.enter_context(tc.psum_pool(name="ps", bufs=1))
+
+        offsets = sb.tile([P, I // 16], U16, name="offsets")
+        nc.sync.dma_start(offsets[:], offs)
+
+        os_slot = sb.tile([P, PACK], F32, name="os_slot")
+        nc.gpsimd.dma_start(out=os_slot[:], in_=slot_factor.rearrange("o (p t) -> (o p) t", t=PACK))
+        relu_x = sb.tile([P, G + 1], F32, name="relu_x")
+        nc.gpsimd.dma_start(out=relu_x[:, G : G + 1], in_=reserve)
+
+        pool_scales = sb.tile([P, T], U8, name="pool_scales", align_bytes=64)
+        nc.vector.memset(pool_scales[:].bitcast(I32), 0)
+        for quad in range(4):
+            nc.sync.dma_start(
+                out=pool_scales[32 * quad : 32 * quad + 4, :].bitcast(I32),
+                in_=keys_scales[0, 4 * quad : 4 * quad + 4, :].bitcast(I32),
+            )
+        pool_words = sb.tile([P, T], U16, name="pool_words", align_bytes=64)
+        nc.sync.dma_start(out=pool_words[:].bitcast(I32), in_=keys_words[0].bitcast(I32))
+
+        sides = (("b", query2), ("tb", dquery2), ("a", query))
+        raw = {}
+        for name, src in sides:
+            raw[name] = sb.tile([P, PACK, Q], F32, name="raw_" + name)
+            nc.sync.dma_start(out=raw[name][:], in_=src.rearrange("(p t) q -> p t q", t=PACK))
+        pool_vals = []
+        for j in range(TILES):
+            pool_vals.append(sb.tile([P, T], F32, name="pool_vals%d" % j))
+            nc.sync.dma_start(out=pool_vals[j][:], in_=vals[j * P : (j + 1) * P, :])
+
+        ident = sb.tile([P, P], F32, name="ident")
+        make_identity(nc, ident[:])
+        log_sig = sb.tile([P, G + 1], F32, name="log_sig")
+        nc.gpsimd.memset(log_sig[:], 0.0)
+
+        key_scales = sb.tile([P, I], U8, name="key_scales", align_bytes=64)
+        nc.vector.tensor_copy(key_scales[:], pool_scales[:].indirect(offsets[:]))
+        key_words = sb.tile([P, I], U16, name="key_words", align_bytes=64)
+        nc.vector.tensor_copy(key_words[:], pool_words[:].indirect(offsets[:]))
+
+        score = {}
+        for name, src in sides:
+            woven = sb.tile([P, Q, PACK], BF16, name="woven_" + name, align_bytes=64)
+            nc.scalar.activation(woven[:], raw[name][:].rearrange("p t q -> p q t"), ACT.Copy)
+            codes = sb.tile([P, Q], U32, name="codes_" + name, align_bytes=64)
+            scales = sb.tile([P, Q], U8, name="scales_" + name, align_bytes=64)
+            nc.vector.quantize_mx(out=codes[:].bitcast(FP8X4), scales=scales[:], in_=woven[:].rearrange("p q t -> p (q t)"))
+            score[name] = ps.tile([P, I], F32, name="score_" + name, tag="bank_" + name)
+            nc.tensor.matmul_mx(
+                out=score[name][:],
+                lhsT=codes[:].bitcast(FP8X4),
+                lhsT_scale=scales[:],
+                rhs=key_words[:].bitcast(FP4X4),
+                rhs_scale=key_scales[:],
+                start=True,
+                stop=True,
+            )
+
+        def pages(bank):
+            return bank[:].rearrange("q (g r) -> q g r", r=PAGE)
+
+        sum_b = sb.tile([P, G], F32, name="sum_b")
+        nc.vector.tensor_reduce(sum_b[:], pages(score["b"]), AX.X, ALU.add)
+        sum_tb = sb.tile([P, G], F32, name="sum_tb")
+        nc.vector.tensor_reduce(sum_tb[:], pages(score["tb"]), AX.X, ALU.add)
+        max_a = sb.tile([P, G], F32, name="max_a")
+        nc.vector.tensor_reduce(max_a[:], pages(score["a"]), AX.X, ALU.max)
+
+        c = 3.0 / PAGE
+        abs_x = sb.tile([P, G], F32, name="abs_x")
+        nc.scalar.activation(abs_x[:], sum_b[:], ACT.Abs, scale=c)
+        neg_x = sb.tile([P, G], F32, name="neg_x")
+        nc.scalar.activation(neg_x[:], sum_b[:], ACT.Relu, scale=-c)
+        nc.scalar.activation(relu_x[:, :G], sum_b[:], ACT.Relu, scale=c)
+        tanh_h = sb.tile([P, G], F32, name="tanh_h")
+        nc.scalar.activation(tanh_h[:], abs_x[:], ACT.Tanh, scale=0.5)
+        exp_min = sb.tile([P, G], F32, name="exp_min")
+        nc.scalar.activation(exp_min[:], neg_x[:], ACT.Exp, scale=-1.0)
+
+        shifted = sb.tile([P, PACK, G, 2], F32, name="shifted")
+        nc.vector.tensor_tensor(
+            shifted[:],
+            score["a"][:].rearrange("q (g h t) -> q t g h", h=2, t=PACK),
+            max_a[:].unsqueeze(1).unsqueeze(3).broadcast_to([P, PACK, G, 2]),
+            ALU.subtract,
+        )
+        pa = sb.tile([P, PACK, G, 2], F32, name="pa")
+        nc.scalar.activation(pa[:], shifted[:], ACT.Exp)
+        nc.scalar.activation(log_sig[:, :G], tanh_h[:], ACT.Ln, scale=0.5, bias=0.5)
+
+        pa_turned = ps.tile([P, PACK, Q], F32, name="pa_turned", tag="bank_pa")
+        for t in range(PACK):
+            nc.tensor.transpose(pa_turned[:, t, :], pa[:, t, :, :].rearrange("q g h -> q (g h)"), ident[:])
+        pa_os = sb.tile([P, PACK, Q], F32, name="pa_os")
+        for t in range(PACK):
+            nc.scalar.activation(pa_os[:, t, :], pa_turned[:, t, :], ACT.Copy, scale=os_slot[:, t : t + 1])
+
+        s = sb.tile([P, G], F32, name="s")
+        nc.vector.tensor_reduce(s[:], pa[:].rearrange("q t g h -> q g t h"), AX.XY, ALU.add)
+        inv_s = sb.tile([P, G], F32, name="inv_s")
+        nc.vector.reciprocal(inv_s[:], s[:])
+
+        sig2 = sb.tile([P, G], F32, name="sig2")
+        nc.vector.scalar_tensor_tensor(sig2[:], tanh_h[:], 1.0, exp_min[:], ALU.add, ALU.mult)
+        neg_tq0 = sb.tile([P, G], F32, name="neg_tq0")
+        neg_tz = sb.tile([P, 1], F32, name="neg_tz")
+        nc.vector.scalar_tensor_tensor(neg_tq0[:], sum_tb[:], -0.5 * c, sig2[:], ALU.mult, ALU.mult, accum_out=neg_tz[:])
+        q0 = sb.tile([P, G + 1], F32, name="q0")
+        z = sb.tile([P, 1], F32, name="z")
+        nc.vector.scalar_tensor_tensor(q0[:], relu_x[:], 1.0, log_sig[:], ALU.mult, ALU.subtract, accum_out=z[:])
+        inv_z = sb.tile([P, 1], F32, name="inv_z")
+        nc.vector.reciprocal(inv_z[:], z[:])
+        ratio = sb.tile([P, 1], F32, name="ratio")
+        nc.vector.tensor_tensor(ratio[:], neg_tz[:], inv_z[:], ALU.mult)
+        change = sb.tile([P, G], F32, name="change")
+        nc.vector.scalar_tensor_tensor(change[:], q0[:, :G], ratio[:], neg_tq0[:], ALU.mult, ALU.subtract)
+        tr = sb.tile([P, G, 2], F32, name="tr")
+        nc.vector.scalar_tensor_tensor(
+            tr[:],
+            change[:].unsqueeze(2).broadcast_to([P, G, 2]),
+            inv_z[:],
+            inv_s[:].unsqueeze(2).broadcast_to([P, G, 2]),
+            ALU.mult,
+            ALU.mult,
+        )
+        tr_turned = ps.tile([P, Q], F32, name="tr_turned", tag="bank_tr")
+        nc.tensor.transpose(tr_turned[:], tr[:].rearrange("q g h -> q (g h)"), ident[:])
+        w_woven = sb.tile([P, Q, PACK], BF16, name="w_woven", align_bytes=64)
+        nc.vector.tensor_tensor(
+            w_woven[:],
+            pa_os[:].rearrange("p t q -> p q t"),
+            tr_turned[:].unsqueeze(2).broadcast_to([P, Q, PACK]),
+            ALU.mult,
+        )
+        w_codes = sb.tile([P, Q], U32, name="w_codes", align_bytes=64)
+        w_scales = sb.tile([P, Q], U8, name="w_scales", align_bytes=64)
+        nc.vector.quantize_mx(out=w_codes[:].bitcast(FP8X4), scales=w_scales[:], in_=w_woven[:].rearrange("p q t -> p (q t)"))
+
+        v_codes, v_scales = [], []
+        for j in range(TILES):
+            picked = sb.tile([P, I], BF16, name="picked%d" % j, align_bytes=64)
+            nc.vector.tensor_copy(picked[:], pool_vals[j][:].indirect(offsets[:]))
+            pairs = picked[:].bitcast(F32)
+            turned = ps.tile([P, 2, P], F32, name="turned%d" % j, tag="bank_v", bufs=2)
+            for u in range(2):
+                nc.tensor.transpose(turned[:, u, :], pairs[:, u : I // 2 : 2], ident[:])
+            v_woven = sb.tile([P, P * PACK], BF16, name="v_woven%d" % j, align_bytes=64)
+            nc.scalar.copy(
+                v_woven[:].bitcast(F32).rearrange("p (e u) -> p e u", u=2),
+                turned[:].rearrange("p u e -> p e u"),
+            )
+            v_codes.append(sb.tile([P, P], U32, name="v_codes%d" % j, align_bytes=64))
+            v_scales.append(sb.tile([P, P], U8, name="v_scales%d" % j, align_bytes=64))
+            nc.vector.quantize_mx(out=v_codes[j][:].bitcast(FP8X4), scales=v_scales[j][:], in_=v_woven[:])
+
+        for tag, first, last in (("bank_b", 0, TILES - 1), ("bank_tb", TILES - 1, TILES)):
+            width = (last - first) * P
+            acc = ps.tile([P, I], F32, name="acc%d" % first, tag=tag)
+            for j in range(first, last):
+                nc.tensor.matmul_mx(
+                    out=acc[:, (j - first) * P : (j - first + 1) * P],
+                    lhsT=w_codes[:].bitcast(FP8X4),
+                    lhsT_scale=w_scales[:],
+                    rhs=v_codes[j][:].bitcast(FP8X4),
+                    rhs_scale=v_scales[j][:],
+                    start=True,
+                    stop=True,
+                )
+            result = sb.tile([P, width], F32, name="result%d" % first)
+            nc.scalar.copy(result[:], acc[:, :width])
+            nc.sync.dma_start(out=out[:, first * P : last * P], in_=result[:])

@@ -28,16 +28,13 @@ def tile_attend_ttpagequotas_kernel(tc, query, query2, keys_words, keys_scales, 
     nc = tc.nc
     with ExitStack() as ctx:
         sb = ctx.enter_context(tc.tile_pool(name="sb", bufs=1))
+        shared = ctx.enter_context(tc.tile_pool(name="shared", bufs=1))
         ps = ctx.enter_context(tc.psum_pool(name="ps", bufs=1))
 
         offsets = sb.tile([P, I // 16], U16, name="offsets")
         nc.sync.dma_start(offsets[:], offs)
-
-        os_slot = sb.tile([P, PACK], F32, name="os_slot")
-        nc.gpsimd.dma_start(out=os_slot[:], in_=slot_factor.rearrange("o (p t) -> (o p) t", t=PACK))
-        relu_x = sb.tile([P, G + 1], F32, name="relu_x")
-        nc.gpsimd.dma_start(out=relu_x[:, G : G + 1], in_=reserve)
-
+        pool_words = sb.tile([P, T], U16, name="pool_words", align_bytes=64)
+        nc.sync.dma_start(out=pool_words[:].bitcast(I32), in_=keys_words[0].bitcast(I32))
         pool_scales = sb.tile([P, T], U8, name="pool_scales", align_bytes=64)
         nc.vector.memset(pool_scales[:].bitcast(I32), 0)
         for quad in range(4):
@@ -45,28 +42,31 @@ def tile_attend_ttpagequotas_kernel(tc, query, query2, keys_words, keys_scales, 
                 out=pool_scales[32 * quad : 32 * quad + 4, :].bitcast(I32),
                 in_=keys_scales[0, 4 * quad : 4 * quad + 4, :].bitcast(I32),
             )
-        pool_words = sb.tile([P, T], U16, name="pool_words", align_bytes=64)
-        nc.sync.dma_start(out=pool_words[:].bitcast(I32), in_=keys_words[0].bitcast(I32))
 
-        sides = (("b", query2), ("tb", dquery2), ("a", query))
+        sides = (("a", query), ("b", query2), ("tb", dquery2))
         raw = {}
         for name, src in sides:
             raw[name] = sb.tile([P, PACK, Q], F32, name="raw_" + name)
             nc.sync.dma_start(out=raw[name][:], in_=src.rearrange("(p t) q -> p t q", t=PACK))
+        relu_x = sb.tile([P, G + 1], F32, name="relu_x")
         pool_vals = []
         for j in range(TILES):
-            pool_vals.append(sb.tile([P, T], F32, name="pool_vals%d" % j))
+            pool_vals.append(shared.tile([P, T], F32, name="pool_vals%d" % j, align_bytes=64, offset=j * T * 4))
             nc.sync.dma_start(out=pool_vals[j][:], in_=vals[j * P : (j + 1) * P, :])
+            if j == 0:
+                nc.sync.dma_start(out=relu_x[:, G : G + 1], in_=reserve)
+                os_slot = sb.tile([P, PACK], F32, name="os_slot")
+                nc.sync.dma_start(out=os_slot[:], in_=slot_factor.rearrange("o (p t) -> (o p) t", t=PACK))
 
-        ident = sb.tile([P, P], F32, name="ident")
-        make_identity(nc, ident[:])
         log_sig = sb.tile([P, G + 1], F32, name="log_sig")
         nc.gpsimd.memset(log_sig[:], 0.0)
+        ident = sb.tile([P, P], F32, name="ident")
+        make_identity(nc, ident[:])
 
-        key_scales = sb.tile([P, I], U8, name="key_scales", align_bytes=64)
-        nc.vector.tensor_copy(key_scales[:], pool_scales[:].indirect(offsets[:]))
         key_words = sb.tile([P, I], U16, name="key_words", align_bytes=64)
         nc.vector.tensor_copy(key_words[:], pool_words[:].indirect(offsets[:]))
+        key_scales = sb.tile([P, I], U8, name="key_scales", align_bytes=64)
+        nc.vector.tensor_copy(key_scales[:], pool_scales[:].indirect(offsets[:]))
 
         score = {}
         for name, src in sides:
@@ -86,15 +86,48 @@ def tile_attend_ttpagequotas_kernel(tc, query, query2, keys_words, keys_scales, 
                 stop=True,
             )
 
+        def behind(j, place, shape, dtype, name):
+            return shared.tile(shape, dtype, name=name, align_bytes=64, offset=j * T * 4 + place * 1024)
+
         def pages(bank):
             return bank[:].rearrange("q (g r) -> q g r", r=PAGE)
 
-        sum_b = sb.tile([P, G], F32, name="sum_b")
-        nc.vector.tensor_reduce(sum_b[:], pages(score["b"]), AX.X, ALU.add)
-        sum_tb = sb.tile([P, G], F32, name="sum_tb")
-        nc.vector.tensor_reduce(sum_tb[:], pages(score["tb"]), AX.X, ALU.add)
+        v_woven, v_codes, v_scales = {}, {}, {}
+
+        def value_tile(j):
+            picked = sb.tile([P, I], BF16, name="picked%d" % j, align_bytes=64)
+            nc.vector.tensor_copy(picked[:], pool_vals[j][:].indirect(offsets[:]))
+            pairs = picked[:].bitcast(F32)
+            turned = ps.tile([P, 2, P], F32, name="turned%d" % j, tag="bank_v", bufs=2)
+            for u in range(2):
+                nc.tensor.transpose(turned[:, u, :], pairs[:, u : I // 2 : 2], ident[:])
+            v_woven[j] = sb.tile([P, I], BF16, name="v_woven%d" % j, align_bytes=64)
+            nc.scalar.copy(
+                v_woven[j][:].bitcast(F32).rearrange("p (e u) -> p e u", u=2),
+                turned[:].rearrange("p u e -> p e u"),
+            )
+
+        def quantise_values(j):
+            half = j // 2
+            if j % 2 == 0:
+                v_codes[half] = behind(j + 1, 4, [P, 2 * P], U32, "v_codes%d" % half)
+                v_scales[half] = sb.tile([P, 2 * P], U8, name="v_scales%d" % half, align_bytes=64)
+            cols = slice(j % 2 * P, (j % 2 + 1) * P)
+            nc.vector.quantize_mx(out=v_codes[half][:, cols].bitcast(FP8X4), scales=v_scales[half][:, cols], in_=v_woven[j][:])
+
         max_a = sb.tile([P, G], F32, name="max_a")
         nc.vector.tensor_reduce(max_a[:], pages(score["a"]), AX.X, ALU.max)
+        sum_b = sb.tile([P, G], F32, name="sum_b")
+        nc.vector.tensor_reduce(sum_b[:], pages(score["b"]), AX.X, ALU.add)
+        shifted = sb.tile([P, PACK, G, 2], F32, name="shifted")
+        nc.vector.tensor_tensor(
+            shifted[:],
+            score["a"][:].rearrange("q (g h t) -> q t g h", h=2, t=PACK),
+            max_a[:].unsqueeze(1).unsqueeze(3).broadcast_to([P, PACK, G, 2]),
+            ALU.subtract,
+        )
+        sum_tb = sb.tile([P, G], F32, name="sum_tb")
+        nc.vector.tensor_reduce(sum_tb[:], pages(score["tb"]), AX.X, ALU.add)
 
         c = 3.0 / PAGE
         abs_x = sb.tile([P, G], F32, name="abs_x")
@@ -105,46 +138,43 @@ def tile_attend_ttpagequotas_kernel(tc, query, query2, keys_words, keys_scales, 
         tanh_h = sb.tile([P, G], F32, name="tanh_h")
         nc.scalar.activation(tanh_h[:], abs_x[:], ACT.Tanh, scale=0.5)
         exp_min = sb.tile([P, G], F32, name="exp_min")
-        nc.scalar.activation(exp_min[:], neg_x[:], ACT.Exp, scale=-1.0)
+        nc.scalar.activation(exp_min[:], neg_x[:], ACT.Exp, scale=-1.0, bias=log_sig[:, 0:1])
 
-        shifted = sb.tile([P, PACK, G, 2], F32, name="shifted")
-        nc.vector.tensor_tensor(
-            shifted[:],
-            score["a"][:].rearrange("q (g h t) -> q t g h", h=2, t=PACK),
-            max_a[:].unsqueeze(1).unsqueeze(3).broadcast_to([P, PACK, G, 2]),
-            ALU.subtract,
-        )
         pa = sb.tile([P, PACK, G, 2], F32, name="pa")
-        nc.scalar.activation(pa[:], shifted[:], ACT.Exp)
+        nc.scalar.activation(pa[:], shifted[:], ACT.Exp, bias=log_sig[:, 0:1])
         nc.scalar.activation(log_sig[:, :G], tanh_h[:], ACT.Ln, scale=0.5, bias=0.5)
 
         pa_turned = ps.tile([P, PACK, Q], F32, name="pa_turned", tag="bank_pa")
         for t in range(PACK):
             nc.tensor.transpose(pa_turned[:, t, :], pa[:, t, :, :].rearrange("q g h -> q (g h)"), ident[:])
-        pa_os = sb.tile([P, PACK, Q], F32, name="pa_os")
-        for t in range(PACK):
-            nc.scalar.activation(pa_os[:, t, :], pa_turned[:, t, :], ACT.Copy, scale=os_slot[:, t : t + 1])
-
-        s = sb.tile([P, G], F32, name="s")
-        nc.vector.tensor_reduce(s[:], pa[:].rearrange("q t g h -> q g t h"), AX.XY, ALU.add)
-        inv_s = sb.tile([P, G], F32, name="inv_s")
-        nc.vector.reciprocal(inv_s[:], s[:])
 
         sig2 = sb.tile([P, G], F32, name="sig2")
         nc.vector.scalar_tensor_tensor(sig2[:], tanh_h[:], 1.0, exp_min[:], ALU.add, ALU.mult)
-        neg_tq0 = sb.tile([P, G], F32, name="neg_tq0")
+        pa_os = sb.tile([P, PACK, Q], F32, name="pa_os")
+        for t in range(PACK):
+            nc.scalar.activation(pa_os[:, t, :], pa_turned[:, t, :], ACT.Copy, scale=os_slot[:, t : t + 1])
+        value_tile(0)
+        s = behind(0, 0, [P, G], F32, "s")
+        nc.vector.tensor_reduce(s[:], pa[:].rearrange("q t g h -> q g t h"), AX.XY, ALU.add)
+        neg_tq0 = behind(0, 1, [P, G], F32, "neg_tq0")
         neg_tz = sb.tile([P, 1], F32, name="neg_tz")
         nc.vector.scalar_tensor_tensor(neg_tq0[:], sum_tb[:], -0.5 * c, sig2[:], ALU.mult, ALU.mult, accum_out=neg_tz[:])
-        q0 = sb.tile([P, G + 1], F32, name="q0")
+        value_tile(1)
+        q0 = behind(1, 0, [P, G + 1], F32, "q0")
         z = sb.tile([P, 1], F32, name="z")
         nc.vector.scalar_tensor_tensor(q0[:], relu_x[:], 1.0, log_sig[:], ALU.mult, ALU.subtract, accum_out=z[:])
+        inv_s = behind(1, 1, [P, G], F32, "inv_s")
+        nc.vector.reciprocal(inv_s[:], s[:])
         inv_z = sb.tile([P, 1], F32, name="inv_z")
         nc.vector.reciprocal(inv_z[:], z[:])
+        quantise_values(0)
         ratio = sb.tile([P, 1], F32, name="ratio")
         nc.vector.tensor_tensor(ratio[:], neg_tz[:], inv_z[:], ALU.mult)
+        quantise_values(1)
         change = sb.tile([P, G], F32, name="change")
         nc.vector.scalar_tensor_tensor(change[:], q0[:, :G], ratio[:], neg_tq0[:], ALU.mult, ALU.subtract)
-        tr = sb.tile([P, G, 2], F32, name="tr")
+        value_tile(2)
+        tr = behind(2, 0, [P, G, 2], F32, "tr")
         nc.vector.scalar_tensor_tensor(
             tr[:],
             change[:].unsqueeze(2).broadcast_to([P, G, 2]),
@@ -155,47 +185,35 @@ def tile_attend_ttpagequotas_kernel(tc, query, query2, keys_words, keys_scales, 
         )
         tr_turned = ps.tile([P, Q], F32, name="tr_turned", tag="bank_tr")
         nc.tensor.transpose(tr_turned[:], tr[:].rearrange("q g h -> q (g h)"), ident[:])
-        w_woven = sb.tile([P, Q, PACK], BF16, name="w_woven", align_bytes=64)
+        value_tile(3)
+        w_woven = behind(3, 0, [P, Q, PACK], BF16, "w_woven")
         nc.vector.tensor_tensor(
             w_woven[:],
             pa_os[:].rearrange("p t q -> p q t"),
             tr_turned[:].unsqueeze(2).broadcast_to([P, Q, PACK]),
             ALU.mult,
         )
+        quantise_values(2)
         w_codes = sb.tile([P, Q], U32, name="w_codes", align_bytes=64)
         w_scales = sb.tile([P, Q], U8, name="w_scales", align_bytes=64)
         nc.vector.quantize_mx(out=w_codes[:].bitcast(FP8X4), scales=w_scales[:], in_=w_woven[:].rearrange("p q t -> p (q t)"))
+        quantise_values(3)
 
-        v_codes, v_scales = [], []
-        for j in range(TILES):
-            picked = sb.tile([P, I], BF16, name="picked%d" % j, align_bytes=64)
-            nc.vector.tensor_copy(picked[:], pool_vals[j][:].indirect(offsets[:]))
-            pairs = picked[:].bitcast(F32)
-            turned = ps.tile([P, 2, P], F32, name="turned%d" % j, tag="bank_v", bufs=2)
-            for u in range(2):
-                nc.tensor.transpose(turned[:, u, :], pairs[:, u : I // 2 : 2], ident[:])
-            v_woven = sb.tile([P, P * PACK], BF16, name="v_woven%d" % j, align_bytes=64)
-            nc.scalar.copy(
-                v_woven[:].bitcast(F32).rearrange("p (e u) -> p e u", u=2),
-                turned[:].rearrange("p u e -> p e u"),
+        for half, tag in enumerate(("bank_b", "bank_tb")):
+            cols = slice(half * 2 * P, (half + 1) * 2 * P)
+            acc = ps.tile([P, I], F32, name="acc%d" % half, tag=tag)
+            nc.tensor.matmul_mx(
+                out=acc[:, : 2 * P],
+                lhsT=w_codes[:].bitcast(FP8X4),
+                lhsT_scale=w_scales[:],
+                rhs=v_codes[half][:].bitcast(FP8X4),
+                rhs_scale=v_scales[half][:],
+                start=True,
+                stop=True,
             )
-            v_codes.append(sb.tile([P, P], U32, name="v_codes%d" % j, align_bytes=64))
-            v_scales.append(sb.tile([P, P], U8, name="v_scales%d" % j, align_bytes=64))
-            nc.vector.quantize_mx(out=v_codes[j][:].bitcast(FP8X4), scales=v_scales[j][:], in_=v_woven[:])
-
-        for tag, first, last in (("bank_b", 0, TILES - 1), ("bank_tb", TILES - 1, TILES)):
-            width = (last - first) * P
-            acc = ps.tile([P, I], F32, name="acc%d" % first, tag=tag)
-            for j in range(first, last):
-                nc.tensor.matmul_mx(
-                    out=acc[:, (j - first) * P : (j - first + 1) * P],
-                    lhsT=w_codes[:].bitcast(FP8X4),
-                    lhsT_scale=w_scales[:],
-                    rhs=v_codes[j][:].bitcast(FP8X4),
-                    rhs_scale=v_scales[j][:],
-                    start=True,
-                    stop=True,
-                )
-            result = sb.tile([P, width], F32, name="result%d" % first)
-            nc.scalar.copy(result[:], acc[:, :width])
-            nc.sync.dma_start(out=out[:, first * P : last * P], in_=result[:])
+            result = sb.tile([P, 2 * P], F32, name="result%d" % half)
+            if half == 0:
+                nc.scalar.copy(result[:], acc[:, : 2 * P])
+            else:
+                nc.vector.tensor_copy(result[:], acc[:, : 2 * P])
+            nc.sync.dma_start(out=out[:, cols], in_=result[:])

@@ -43,7 +43,7 @@ def tile_attend_ttpagequotas_kernel(tc, query, query2, keys_words, keys_scales, 
                 in_=keys_scales[0, 4 * quad : 4 * quad + 4, :].bitcast(I32),
             )
 
-        sides = (("a", query), ("b", query2), ("tb", dquery2))
+        sides = (("a", query), ("tb", dquery2), ("b", query2))
         raw = {}
         for name, src in sides:
             raw[name] = sb.tile([P, PACK, Q], F32, name="raw_" + name)
@@ -70,7 +70,7 @@ def tile_attend_ttpagequotas_kernel(tc, query, query2, keys_words, keys_scales, 
 
         score = {}
         for name, src in sides:
-            woven = sb.tile([P, Q, PACK], BF16, name="woven_" + name, align_bytes=64)
+            woven = sb.tile([P, Q, PACK], BF16, name="woven_" + name, tag="woven_" + name, align_bytes=64)
             nc.scalar.activation(woven[:], raw[name][:].rearrange("p t q -> p q t"), ACT.Copy)
             codes = sb.tile([P, Q], U32, name="codes_" + name, align_bytes=64)
             scales = sb.tile([P, Q], U8, name="scales_" + name, align_bytes=64)
@@ -92,16 +92,19 @@ def tile_attend_ttpagequotas_kernel(tc, query, query2, keys_words, keys_scales, 
         def pages(bank):
             return bank[:].rearrange("q (g r) -> q g r", r=PAGE)
 
-        v_woven, v_codes, v_scales = {}, {}, {}
+        gathered, v_woven, v_codes, v_scales = {}, {}, {}, {}
 
         def value_tile(j):
-            picked = sb.tile([P, I], BF16, name="picked%d" % j, align_bytes=64)
+            picked = sb.tile([P, I], BF16, name="picked%d" % j, tag="woven_b" if j == 0 else "picked%d" % j, align_bytes=64)
             nc.vector.tensor_copy(picked[:], pool_vals[j][:].indirect(offsets[:]))
-            pairs = picked[:].bitcast(F32)
+            gathered[j] = picked
+
+        def turn_values(j):
+            pairs = gathered[j][:].bitcast(F32)
             turned = ps.tile([P, 2, P], F32, name="turned%d" % j, tag="bank_v", bufs=2)
             for u in range(2):
                 nc.tensor.transpose(turned[:, u, :], pairs[:, u : I // 2 : 2], ident[:])
-            v_woven[j] = sb.tile([P, I], BF16, name="v_woven%d" % j, align_bytes=64)
+            v_woven[j] = shared.tile([P, I], BF16, name="v_woven%d" % j, align_bytes=64, offset=TILES * T * 4 + 2048 + j * I * 2)
             nc.scalar.copy(
                 v_woven[j][:].bitcast(F32).rearrange("p (e u) -> p e u", u=2),
                 turned[:].rearrange("p u e -> p e u"),
@@ -110,24 +113,39 @@ def tile_attend_ttpagequotas_kernel(tc, query, query2, keys_words, keys_scales, 
         def quantise_values(j):
             half = j // 2
             if j % 2 == 0:
-                v_codes[half] = behind(j + 1, 4, [P, 2 * P], U32, "v_codes%d" % half)
+                v_codes[half] = behind(half + 2, 4, [P, 2 * P], U32, "v_codes%d" % half)
                 v_scales[half] = sb.tile([P, 2 * P], U8, name="v_scales%d" % half, align_bytes=64)
             cols = slice(j % 2 * P, (j % 2 + 1) * P)
             nc.vector.quantize_mx(out=v_codes[half][:, cols].bitcast(FP8X4), scales=v_scales[half][:, cols], in_=v_woven[j][:])
 
-        max_a = sb.tile([P, G], F32, name="max_a")
+        def dealt(bank):
+            return bank[:].rearrange("q (g h t) -> q t g h", h=2, t=PACK)
+
+        max_a = sb.tile([P, G], F32, name="max_a", tag="woven_b", align_bytes=64)
         nc.vector.tensor_reduce(max_a[:], pages(score["a"]), AX.X, ALU.max)
-        sum_b = sb.tile([P, G], F32, name="sum_b")
-        nc.vector.tensor_reduce(sum_b[:], pages(score["b"]), AX.X, ALU.add)
         shifted = sb.tile([P, PACK, G, 2], F32, name="shifted")
         nc.vector.tensor_tensor(
             shifted[:],
-            score["a"][:].rearrange("q (g h t) -> q t g h", h=2, t=PACK),
+            dealt(score["a"]),
             max_a[:].unsqueeze(1).unsqueeze(3).broadcast_to([P, PACK, G, 2]),
             ALU.subtract,
         )
-        sum_tb = sb.tile([P, G], F32, name="sum_tb")
-        nc.vector.tensor_reduce(sum_tb[:], pages(score["tb"]), AX.X, ALU.add)
+        sum_b = sb.tile([P, G], F32, name="sum_b")
+        nc.vector.tensor_reduce(sum_b[:], pages(score["b"]), AX.X, ALU.add)
+
+        terms = sb.tile([P, PACK, 2, G, 2], F32, name="terms")
+        nc.scalar.copy(terms[:, :, 0, :, :], dealt(score["tb"]))
+        nc.scalar.activation(terms[:, :, 1, :, :], shifted[:], ACT.Exp, bias=log_sig[:, 0:1])
+        sums_turned = ps.tile([P, Q], F32, name="sums_turned", tag="bank_tb")
+        for r in range(PAGE):
+            nc.tensor.matmul(
+                sums_turned[:],
+                lhsT=terms[:, r % PACK, :, :, r // PACK].rearrange("q side g -> q (side g)"),
+                rhs=ident[:],
+                is_transpose=True,
+                start=(r == 0),
+                stop=(r == PAGE - 1),
+            )
 
         c = 3.0 / PAGE
         abs_x = sb.tile([P, G], F32, name="abs_x")
@@ -135,46 +153,52 @@ def tile_attend_ttpagequotas_kernel(tc, query, query2, keys_words, keys_scales, 
         neg_x = sb.tile([P, G], F32, name="neg_x")
         nc.scalar.activation(neg_x[:], sum_b[:], ACT.Relu, scale=-c)
         nc.scalar.activation(relu_x[:, :G], sum_b[:], ACT.Relu, scale=c)
-        tanh_h = sb.tile([P, G], F32, name="tanh_h")
+        tanh_h = shared.tile([P, G], F32, name="tanh_h", align_bytes=64, offset=TILES * T * 4 + 1536 + 384)
         nc.scalar.activation(tanh_h[:], abs_x[:], ACT.Tanh, scale=0.5)
         exp_min = sb.tile([P, G], F32, name="exp_min")
         nc.scalar.activation(exp_min[:], neg_x[:], ACT.Exp, scale=-1.0, bias=log_sig[:, 0:1])
 
-        pa = sb.tile([P, PACK, G, 2], F32, name="pa")
-        nc.scalar.activation(pa[:], shifted[:], ACT.Exp, bias=log_sig[:, 0:1])
         nc.scalar.activation(log_sig[:, :G], tanh_h[:], ACT.Ln, scale=0.5, bias=0.5)
+
+        value_tile(0)
+        sig2 = behind(0, 0, [P, G], F32, "sig2")
+        nc.vector.scalar_tensor_tensor(sig2[:], tanh_h[:], 1.0, exp_min[:], ALU.add, ALU.mult)
+        sums_staged = shared.tile([P, Q], F32, name="sums_staged", align_bytes=64, offset=TILES * T * 4 + 1536)
+        nc.scalar.copy(sums_staged[:], sums_turned[:])
+        sums = ps.tile([P, 2 * G], F32, name="sums", tag="bank_a")
+        nc.tensor.transpose(sums[:], sums_staged[:], ident[:])
 
         pa_turned = ps.tile([P, PACK, Q], F32, name="pa_turned", tag="bank_pa")
         for t in range(PACK):
-            nc.tensor.transpose(pa_turned[:, t, :], pa[:, t, :, :].rearrange("q g h -> q (g h)"), ident[:])
+            nc.tensor.transpose(pa_turned[:, t, :], terms[:, t, 1, :, :].rearrange("q g h -> q (g h)"), ident[:])
 
-        sig2 = sb.tile([P, G], F32, name="sig2")
-        nc.vector.scalar_tensor_tensor(sig2[:], tanh_h[:], 1.0, exp_min[:], ALU.add, ALU.mult)
-        pa_os = sb.tile([P, PACK, Q], F32, name="pa_os")
+        turn_values(0)
+        value_tile(1)
+        turn_values(1)
+        pa_os = shared.tile([P, PACK, Q], F32, name="pa_os", align_bytes=64, offset=TILES * T * 4)
         for t in range(PACK):
             nc.scalar.activation(pa_os[:, t, :], pa_turned[:, t, :], ACT.Copy, scale=os_slot[:, t : t + 1])
-        value_tile(0)
-        s = behind(0, 0, [P, G], F32, "s")
-        nc.vector.tensor_reduce(s[:], pa[:].rearrange("q t g h -> q g t h"), AX.XY, ALU.add)
-        neg_tq0 = behind(0, 1, [P, G], F32, "neg_tq0")
-        neg_tz = sb.tile([P, 1], F32, name="neg_tz")
-        nc.vector.scalar_tensor_tensor(neg_tq0[:], sum_tb[:], -0.5 * c, sig2[:], ALU.mult, ALU.mult, accum_out=neg_tz[:])
-        value_tile(1)
-        q0 = behind(1, 0, [P, G + 1], F32, "q0")
+        pa_os_woven = sb.tile([P, Q, PACK], F32, name="pa_os_woven")
+        nc.scalar.copy(pa_os_woven[:], pa_os[:].rearrange("p t q -> p q t"))
+        value_tile(2)
+        turn_values(2)
+        q0 = behind(2, 2, [P, G + 1], F32, "q0")
         z = sb.tile([P, 1], F32, name="z")
         nc.vector.scalar_tensor_tensor(q0[:], relu_x[:], 1.0, log_sig[:], ALU.mult, ALU.subtract, accum_out=z[:])
-        inv_s = behind(1, 1, [P, G], F32, "inv_s")
-        nc.vector.reciprocal(inv_s[:], s[:])
+        neg_tq0 = behind(2, 0, [P, G], F32, "neg_tq0")
+        neg_tz = sb.tile([P, 1], F32, name="neg_tz")
+        nc.vector.scalar_tensor_tensor(neg_tq0[:], sums[:, :G], -0.5 * c, sig2[:], ALU.mult, ALU.mult, accum_out=neg_tz[:])
         inv_z = sb.tile([P, 1], F32, name="inv_z")
         nc.vector.reciprocal(inv_z[:], z[:])
-        quantise_values(0)
+        inv_s = behind(2, 1, [P, G], F32, "inv_s")
+        nc.vector.reciprocal(inv_s[:], sums[:, G:])
         ratio = sb.tile([P, 1], F32, name="ratio")
         nc.vector.tensor_tensor(ratio[:], neg_tz[:], inv_z[:], ALU.mult)
-        quantise_values(1)
+        quantise_values(0)
         change = sb.tile([P, G], F32, name="change")
         nc.vector.scalar_tensor_tensor(change[:], q0[:, :G], ratio[:], neg_tq0[:], ALU.mult, ALU.subtract)
-        value_tile(2)
-        tr = behind(2, 0, [P, G, 2], F32, "tr")
+        quantise_values(1)
+        tr = sb.tile([P, G, 2], F32, name="tr")
         nc.vector.scalar_tensor_tensor(
             tr[:],
             change[:].unsqueeze(2).broadcast_to([P, G, 2]),
@@ -186,10 +210,11 @@ def tile_attend_ttpagequotas_kernel(tc, query, query2, keys_words, keys_scales, 
         tr_turned = ps.tile([P, Q], F32, name="tr_turned", tag="bank_tr")
         nc.tensor.transpose(tr_turned[:], tr[:].rearrange("q g h -> q (g h)"), ident[:])
         value_tile(3)
+        turn_values(3)
         w_woven = behind(3, 0, [P, Q, PACK], BF16, "w_woven")
         nc.vector.tensor_tensor(
             w_woven[:],
-            pa_os[:].rearrange("p t q -> p q t"),
+            pa_os_woven[:],
             tr_turned[:].unsqueeze(2).broadcast_to([P, Q, PACK]),
             ALU.mult,
         )

from contextlib import ExitStack

import concourse.mybir as mybir
from concourse.masks import make_identity

D, E, T, I, Q, G = 512, 512, 2048, 512, 128, 64
FLOPS = 2 * Q * I * D * 3 + 2 * Q * I * E

F32 = mybir.dt.float32
BF16 = mybir.dt.bfloat16
I32 = mybir.dt.int32
U32 = mybir.dt.uint32
U16 = mybir.dt.uint16
U8 = mybir.dt.uint8
FP8X4 = mybir.dt.float8_e4m3fn_x4
FP4X4 = mybir.dt.float4_e2m1fn_x4
ACT = mybir.ActivationFunctionType
ALU = mybir.AluOpType
AX = mybir.AxisListType

P = 128
PACK = 4
PAGE = I // G
TILES = E // P


def tile_attend_ttpagequotas_kernel(tc, query, query2, keys_words, keys_scales, reserve, dquery2, slot_factor, vals, offs, out):
    nc = tc.nc
    with ExitStack() as ctx:
        sb = ctx.enter_context(tc.tile_pool(name="sb", bufs=1))
        shared = ctx.enter_context(tc.tile_pool(name="shared", bufs=1))
        ps = ctx.enter_context(tc.psum_pool(name="ps", bufs=1))

        offsets = sb.tile([P, I // 16], U16, name="offsets")
        nc.sync.dma_start(offsets[:], offs)
        pool_words = sb.tile([P, T], U16, name="pool_words", align_bytes=64)
        nc.sync.dma_start(out=pool_words[:].bitcast(I32), in_=keys_words[0].bitcast(I32))
        pool_scales = sb.tile([P, T], U8, name="pool_scales", align_bytes=64)
        nc.vector.memset(pool_scales[:].bitcast(I32), 0)
        for quad in range(4):
            nc.sync.dma_start(
                out=pool_scales[32 * quad : 32 * quad + 4, :].bitcast(I32),
                in_=keys_scales[0, 4 * quad : 4 * quad + 4, :].bitcast(I32),
            )

        sides = (("a", query), ("tb", dquery2), ("b", query2))
        raw = {}
        for name, src in sides:
            raw[name] = sb.tile([P, PACK, Q], F32, name="raw_" + name)
            nc.sync.dma_start(out=raw[name][:], in_=src.rearrange("(p t) q -> p t q", t=PACK))
        relu_x = sb.tile([P, G + 1], F32, name="relu_x")
        pool_vals = []
        for j in range(TILES):
            pool_vals.append(shared.tile([P, T], F32, name="pool_vals%d" % j, align_bytes=64, offset=j * T * 4))
            nc.sync.dma_start(out=pool_vals[j][:], in_=vals[j * P : (j + 1) * P, :])
            if j == 0:
                nc.sync.dma_start(out=relu_x[:, G : G + 1], in_=reserve)
                os_slot = sb.tile([P, PACK], F32, name="os_slot")
                nc.sync.dma_start(out=os_slot[:], in_=slot_factor.rearrange("o (p t) -> (o p) t", t=PACK))

        log_sig = sb.tile([P, G + 1], F32, name="log_sig")
        nc.gpsimd.memset(log_sig[:], 0.0)
        ident = sb.tile([P, P], F32, name="ident")
        make_identity(nc, ident[:])

        key_words = sb.tile([P, I], U16, name="key_words", align_bytes=64)
        nc.vector.tensor_copy(key_words[:], pool_words[:].indirect(offsets[:]))
        key_scales = sb.tile([P, I], U8, name="key_scales", align_bytes=64)
        nc.vector.tensor_copy(key_scales[:], pool_scales[:].indirect(offsets[:]))

        score = {}
        for name, src in sides:
            woven = sb.tile([P, Q, PACK], BF16, name="woven_" + name, tag="woven_" + name, align_bytes=64)
            nc.scalar.activation(woven[:], raw[name][:].rearrange("p t q -> p q t"), ACT.Copy)
            codes = sb.tile([P, Q], U32, name="codes_" + name, align_bytes=64)
            scales = sb.tile([P, Q], U8, name="scales_" + name, align_bytes=64)
            nc.vector.quantize_mx(out=codes[:].bitcast(FP8X4), scales=scales[:], in_=woven[:].rearrange("p q t -> p (q t)"))
            score[name] = ps.tile([P, I], F32, name="score_" + name, tag="bank_" + name)
            nc.tensor.matmul_mx(
                out=score[name][:],
                lhsT=codes[:].bitcast(FP8X4),
                lhsT_scale=scales[:],
                rhs=key_words[:].bitcast(FP4X4),
                rhs_scale=key_scales[:],
                start=True,
                stop=True,
            )

        def behind(j, place, shape, dtype, name):
            return shared.tile(shape, dtype, name=name, align_bytes=64, offset=j * T * 4 + place * 1024)

        def pages(bank):
            return bank[:].rearrange("q (g r) -> q g r", r=PAGE)

        gathered, v_woven, v_codes, v_scales = {}, {}, {}, {}

        def value_tile(j):
            picked = sb.tile([P, I], BF16, name="picked%d" % j, tag="woven_b" if j == 0 else "picked%d" % j, align_bytes=64)
            nc.vector.tensor_copy(picked[:], pool_vals[j][:].indirect(offsets[:]))
            gathered[j] = picked

        def turn_values(j):
            pairs = gathered[j][:].bitcast(F32)
            turned = ps.tile([P, 2, P], F32, name="turned%d" % j, tag="bank_v", bufs=2)
            for u in range(2):
                nc.tensor.transpose(turned[:, u, :], pairs[:, u : I // 2 : 2], ident[:])
            v_woven[j] = shared.tile([P, I], BF16, name="v_woven%d" % j, align_bytes=64, offset=TILES * T * 4 + 2048 + j * I * 2)
            nc.scalar.copy(
                v_woven[j][:].bitcast(F32).rearrange("p (e u) -> p e u", u=2),
                turned[:].rearrange("p u e -> p e u"),
            )

        def quantise_values(j):
            half = j // 2
            if j % 2 == 0:
                v_codes[half] = behind(half + 2, 4, [P, 2 * P], U32, "v_codes%d" % half)
                v_scales[half] = sb.tile([P, 2 * P], U8, name="v_scales%d" % half, align_bytes=64)
            cols = slice(j % 2 * P, (j % 2 + 1) * P)
            nc.vector.quantize_mx(out=v_codes[half][:, cols].bitcast(FP8X4), scales=v_scales[half][:, cols], in_=v_woven[j][:])

        def dealt(bank):
            return bank[:].rearrange("q (g h t) -> q t g h", h=2, t=PACK)

        max_a = sb.tile([P, G], F32, name="max_a", tag="woven_b", align_bytes=64)
        nc.vector.tensor_reduce(max_a[:], pages(score["a"]), AX.X, ALU.max)
        shifted = sb.tile([P, PACK, G, 2], F32, name="shifted")
        nc.vector.tensor_tensor(
            shifted[:],
            dealt(score["a"]),
            max_a[:].unsqueeze(1).unsqueeze(3).broadcast_to([P, PACK, G, 2]),
            ALU.subtract,
        )
        sum_b = sb.tile([P, G], F32, name="sum_b")
        nc.vector.tensor_reduce(sum_b[:], pages(score["b"]), AX.X, ALU.add)

        terms = sb.tile([P, PACK, 2, G, 2], F32, name="terms")
        nc.scalar.copy(terms[:, :, 0, :, :], dealt(score["tb"]))
        nc.scalar.activation(terms[:, :, 1, :, :], shifted[:], ACT.Exp, bias=log_sig[:, 0:1])
        sums_turned = ps.tile([P, Q], F32, name="sums_turned", tag="bank_tb")
        for r in range(PAGE):
            nc.tensor.matmul(
                sums_turned[:],
                lhsT=terms[:, r % PACK, :, :, r // PACK].rearrange("q side g -> q (side g)"),
                rhs=ident[:],
                is_transpose=True,
                start=(r == 0),
                stop=(r == PAGE - 1),
            )

        c = 3.0 / PAGE
        abs_x = sb.tile([P, G], F32, name="abs_x")
        nc.scalar.activation(abs_x[:], sum_b[:], ACT.Abs, scale=c)
        neg_x = sb.tile([P, G], F32, name="neg_x")
        nc.scalar.activation(neg_x[:], sum_b[:], ACT.Relu, scale=-c)
        nc.scalar.activation(relu_x[:, :G], sum_b[:], ACT.Relu, scale=c)
        tanh_h = shared.tile([P, G], F32, name="tanh_h", align_bytes=64, offset=TILES * T * 4 + 1536 + 384)
        nc.scalar.activation(tanh_h[:], abs_x[:], ACT.Tanh, scale=0.5)
        exp_min = sb.tile([P, G], F32, name="exp_min")
        nc.scalar.activation(exp_min[:], neg_x[:], ACT.Exp, scale=-1.0, bias=log_sig[:, 0:1])

        nc.scalar.activation(log_sig[:, :G], tanh_h[:], ACT.Ln, scale=0.5, bias=0.5)

        value_tile(0)
        sig2 = behind(0, 0, [P, G], F32, "sig2")
        nc.vector.scalar_tensor_tensor(sig2[:], tanh_h[:], 1.0, exp_min[:], ALU.add, ALU.mult)
        sums_staged = shared.tile([P, Q], F32, name="sums_staged", align_bytes=64, offset=TILES * T * 4 + 1536)
        nc.scalar.copy(sums_staged[:], sums_turned[:])
        sums = ps.tile([P, 2 * G], F32, name="sums", tag="bank_a")
        nc.tensor.transpose(sums[:], sums_staged[:], ident[:])

        pa_turned = ps.tile([P, PACK, Q], F32, name="pa_turned", tag="bank_pa")
        for t in range(PACK):
            nc.tensor.transpose(pa_turned[:, t, :], terms[:, t, 1, :, :].rearrange("q g h -> q (g h)"), ident[:])

        turn_values(0)
        value_tile(1)
        turn_values(1)
        pa_os = shared.tile([P, PACK, Q], F32, name="pa_os", align_bytes=64, offset=TILES * T * 4)
        for t in range(PACK):
            nc.scalar.activation(pa_os[:, t, :], pa_turned[:, t, :], ACT.Copy, scale=os_slot[:, t : t + 1])
        pa_os_woven = sb.tile([P, Q, PACK], F32, name="pa_os_woven")
        nc.scalar.copy(pa_os_woven[:], pa_os[:].rearrange("p t q -> p q t"))
        value_tile(2)
        turn_values(2)
        q0 = behind(2, 2, [P, G + 1], F32, "q0")
        z = sb.tile([P, 1], F32, name="z")
        nc.vector.scalar_tensor_tensor(q0[:], relu_x[:], 1.0, log_sig[:], ALU.mult, ALU.subtract, accum_out=z[:])
        neg_tq0 = behind(2, 0, [P, G], F32, "neg_tq0")
        neg_tz = sb.tile([P, 1], F32, name="neg_tz")
        nc.vector.scalar_tensor_tensor(neg_tq0[:], sums[:, :G], -0.5 * c, sig2[:], ALU.mult, ALU.mult, accum_out=neg_tz[:])
        inv_z = sb.tile([P, 1], F32, name="inv_z")
        nc.vector.reciprocal(inv_z[:], z[:])
        inv_s = behind(2, 1, [P, G], F32, "inv_s")
        nc.vector.reciprocal(inv_s[:], sums[:, G:])
        ratio = sb.tile([P, 1], F32, name="ratio")
        nc.vector.tensor_tensor(ratio[:], neg_tz[:], inv_z[:], ALU.mult)
        quantise_values(0)
        change = sb.tile([P, G], F32, name="change")
        nc.vector.scalar_tensor_tensor(change[:], q0[:, :G], ratio[:], neg_tq0[:], ALU.mult, ALU.subtract)
        quantise_values(1)
        tr = sb.tile([P, G, 2], F32, name="tr")
        nc.vector.scalar_tensor_tensor(
            tr[:],
            change[:].unsqueeze(2).broadcast_to([P, G, 2]),
            inv_z[:],
            inv_s[:].unsqueeze(2).broadcast_to([P, G, 2]),
            ALU.mult,
            ALU.mult,
        )
        tr_turned = ps.tile([P, Q], F32, name="tr_turned", tag="bank_tr")
        nc.tensor.transpose(tr_turned[:], tr[:].rearrange("q g h -> q (g h)"), ident[:])
        value_tile(3)
        turn_values(3)
        w_woven = behind(3, 0, [P, Q, PACK], BF16, "w_woven")
        nc.vector.tensor_tensor(
            w_woven[:],
            pa_os_woven[:],
            tr_turned[:].unsqueeze(2).broadcast_to([P, Q, PACK]),
            ALU.mult,
        )
        quantise_values(2)
        w_codes = sb.tile([P, Q], U32, name="w_codes", align_bytes=64)
        w_scales = sb.tile([P, Q], U8, name="w_scales", align_bytes=64)
        nc.vector.quantize_mx(out=w_codes[:].bitcast(FP8X4), scales=w_scales[:], in_=w_woven[:].rearrange("p q t -> p (q t)"))
        quantise_values(3)

        for half, tag in enumerate(("bank_b", "bank_tb")):
            cols = slice(half * 2 * P, (half + 1) * 2 * P)
            acc = ps.tile([P, I], F32, name="acc%d" % half, tag=tag)
            nc.tensor.matmul_mx(
                out=acc[:, : 2 * P],
                lhsT=w_codes[:].bitcast(FP8X4),
                lhsT_scale=w_scales[:],
                rhs=v_codes[half][:].bitcast(FP8X4),
                rhs_scale=v_scales[half][:],
                start=True,
                stop=True,
            )
            result = sb.tile([P, 2 * P], F32, name="result%d" % half)
            if half == 0:
                nc.scalar.copy(result[:], acc[:, : 2 * P])
            else:
                nc.vector.tensor_copy(result[:], acc[:, : 2 * P])
            nc.sync.dma_start(out=out[:, cols], in_=result[:])
